import numpy as np
import ml_dtypes


def mxq(x, axis, fmt="e4m3"):
    dtype, down = {"e4m3": (ml_dtypes.float8_e4m3fn, 7), "e5m2": (ml_dtypes.float8_e5m2, 14)}[fmt]
    v = np.moveaxis(np.asarray(x, np.float32).astype(ml_dtypes.bfloat16).astype(np.float64), axis, -1)
    blocks = v.reshape(v.shape[:-1] + (-1, 32))
    amax = np.abs(blocks).max(-1, keepdims=True)
    byte = np.maximum(np.where(amax > 0, np.frexp(amax)[1] - 1 + 127, 0) - down, 1)
    scale = np.exp2(byte - 127.0)
    codes = (blocks / scale).astype(np.float32).astype(dtype).astype(np.float64)
    return np.moveaxis((codes * scale).reshape(v.shape), -1, axis)


WIDE = False


def mx_kscale(k):
    if not WIDE:
        return np.ones(k)
    levels = np.array([10, -10, 5, -5, 0])
    if k % 512:
        return np.exp2(np.random.permutation(np.resize(levels, k // 32))).repeat(32)
    a = np.empty((k // 512, 16))
    for p in range(k // 512):
        a[p, :8] = np.random.permutation(np.resize(levels, 8))
        for g in range(8):
            far = levels[np.abs(levels - a[p, g]) >= 10]
            a[p, g + 8] = far[np.random.randint(len(far))]
    return np.exp2(a.ravel()).repeat(32)


def f64(x):
    return np.asarray(x).astype(np.float64)


def striped(idx):
    return np.tile(idx.reshape(-1, 16).T, (8, 1)).astype(np.uint16)


def unstriped(offs):
    return offs[:16].T.reshape(-1).astype(np.int64)


E2M1 = np.array([0.0, 0.5, 1.0, 1.5, 2.0, 3.0, 4.0, 6.0, -0.0, -0.5, -1.0, -1.5, -2.0, -3.0, -4.0, -6.0])


def pack_weight(w, fmt):
    k, n = w.shape
    w = f64(np.asarray(w, np.float32).astype(ml_dtypes.bfloat16)).reshape(k // 32, 32, n)
    amax = np.abs(w).max(1)
    if fmt == "e4m3":
        byte = np.frexp(amax)[1] - 1 + 127 - 7
    else:
        mant, ex = np.frexp(amax / 6.0)
        byte = np.where(mant > 0.5, ex, ex - 1) + 127
    byte = np.clip(np.where(amax > 0, byte, 1), 1, 254)
    scaled = (w * np.exp2(127.0 - byte)[:, None, :]).reshape(k, n).astype(np.float32)
    by_word = np.ascontiguousarray(scaled.reshape(k // 512, 128, 4, n).transpose(0, 1, 3, 2))
    if fmt == "e4m3":
        words = by_word.astype(ml_dtypes.float8_e4m3fn).view(np.uint8)
    else:
        c = by_word.astype(ml_dtypes.float4_e2m1fn).view(np.uint8) & 0xF
        words = (c[..., 0::2] | (c[..., 1::2] << 4)).reshape(k // 512, 128, 2 * n)
    return np.ascontiguousarray(words), np.ascontiguousarray(byte.astype(np.uint8).reshape(k // 512, 16, n))


def unpack_weight(words, scales, fmt):
    g, _, n = scales.shape
    words = np.ascontiguousarray(words).reshape(g, 128, n, -1)
    if fmt == "e4m3":
        vals = words.view(ml_dtypes.float8_e4m3fn).astype(np.float64)
    else:
        nib = np.empty((g, 128, n, 4), np.uint8)
        nib[..., 0::2] = words & 0xF
        nib[..., 1::2] = words >> 4
        vals = E2M1[nib]
    vals = vals * np.repeat(np.exp2(scales.astype(np.float64) - 127.0), 8, axis=1)[..., None]
    return vals.transpose(0, 1, 3, 2).reshape(g * 512, n)


def gelu(v):
    return 0.5 * v * (1.0 + np.tanh(np.sqrt(2.0 / np.pi) * (v + 0.044715 * v**3)))


K, T, S, P, H, N = 1024, 2048, 1024, 512, 1024, 512

def setup_inputs():
    n = np.random.standard_normal
    s = mx_kscale(K)[:, None]
    u = mx_kscale(H)[:, None]
    tab_words, tab_scales = pack_weight(n((K, T)) * s, "e4m3")
    w2_words, w2_scales = pack_weight(0.85 * n((K, H)) / np.sqrt(K) / s, "e2m1")
    w4_words, w4_scales = pack_weight(n((H, N)) / np.sqrt(H) / u, "e4m3")
    return {
        "tab_words": tab_words, "tab_scales": tab_scales,
        "offs": striped(np.random.permutation(T)[:S]),
        "pos1": striped(np.random.permutation(S)[:P]),
        "pos2": striped(np.random.permutation(S)[:P]),
        "w1": (0.85 * n((K, H)) / np.sqrt(K) / s).astype(np.float32),
        "w2_words": w2_words, "w2_scales": w2_scales,
        "steep": np.random.uniform(1, 3, H).astype(np.float32),
        "share": np.random.uniform(0.1, 0.5, H).astype(np.float32),
        "age": (2.0 * n((H, P)) * u).astype(np.float32),
        "lean": (np.random.uniform(0.5, 1.2, H) * np.sign(n(H)) * u[:, 0]).astype(np.float32),
        "w3": (n((H, N)) / np.sqrt(H) / u).astype(np.float32),
        "w4_words": w4_words, "w4_scales": w4_scales,
        "resid": (0.6 * n((N, P))).astype(np.float32),
    }

def reference(tab_words, tab_scales, offs, pos1, pos2, w1, w2_words, w2_scales, steep, share, age, lean, w3, w4_words, w4_scales, resid):
    v = unpack_weight(tab_words, tab_scales, "e4m3")[:, unstriped(offs)]
    w2 = unpack_weight(w2_words, w2_scales, "e2m1")
    w4 = unpack_weight(w4_words, w4_scales, "e4m3")
    h = mxq(f64(w1), 0, "e4m3").T @ v
    g = w2.T @ v
    top = h.max(axis=1)
    a = 1.0 / (1.0 + np.exp(-f64(steep)[:, None] * (h[:, unstriped(pos1)] - f64(share)[:, None] * top[:, None])))
    x = a * f64(age) + f64(lean)[:, None] * g[:, unstriped(pos2)]
    xq = mxq(x, 0, "e4m3")
    y = mxq(f64(w3), 0, "e4m3").T @ xq
    d = w4.T @ xq
    return np.maximum(y, d) - f64(resid)

@@ -1,0 +1,313 @@
+from contextlib import ExitStack
+
+import concourse.mybir as mybir
+
+K, T, S, M, H, N = 1024, 2048, 1024, 512, 1024, 512
+FLOPS = 2 * (2 * K * H * S + 2 * H * N * M)
+
+F32 = mybir.dt.float32
+BF16 = mybir.dt.bfloat16
+I32 = mybir.dt.int32
+U32 = mybir.dt.uint32
+U16 = mybir.dt.uint16
+U8 = mybir.dt.uint8
+FP8X4 = mybir.dt.float8_e4m3fn_x4
+FP4X4 = mybir.dt.float4_e2m1fn_x4
+ALU = mybir.AluOpType
+ACT = mybir.ActivationFunctionType
+
+P = 128
+PACK = 4
+PASS = P * PACK
+BANK = 512
+LANES = 16
+WIDE = 384
+
+
+def tile_list_bone_age_evidence_kernel(
+    tc, tab_words, tab_scales, offs, pos1, pos2, w1, w2_words, w2_scales, steep, share, age, lean,
+    w3, w4_words, w4_scales, resid, out,
+):
+    nc = tc.nc
+    with ExitStack() as ctx:
+        lists = ctx.enter_context(tc.tile_pool(name="lists", bufs=1))
+        keep = ctx.enter_context(tc.tile_pool(name="keep", bufs=1))
+        psum = ctx.enter_context(tc.psum_pool(name="psum", bufs=4))
+
+        def held(name, shape, dtype):
+            return keep.tile(shape, dtype, name=name, align_bytes=64)
+
+        def ring(tag, bufs, name, shape, dtype):
+            return keep.tile(shape, dtype, name=name, tag=tag, bufs=bufs, align_bytes=64)
+
+        def bank(tag, name):
+            return psum.tile([P, BANK], F32, name=name, tag=tag)
+
+        offs_sb = lists.tile([P, S // LANES], U16, name="offs_sb")
+        pos1_sb = lists.tile([P, M // LANES], U16, name="pos1_sb")
+        pos2_sb = lists.tile([P, M // LANES], U16, name="pos2_sb")
+
+        tab_w = [held("tab_w%d" % a, [P, T], U32) for a in range(2)]
+        tab_s = ring("first", 1, "tab_s", [P, T], U8)
+        v_s = held("v_s", [P, S], U8)
+        v_s1 = held("v_s1", [P, S], U8)
+        w2_raw = held("w2_raw", [P, 2, 2 * H], U8)
+        w2s_raw = held("w2s_raw", [P, 2, H], U8)
+        w4_w = held("w4_w", [P, 2, N], U32)
+        w4_s = held("w4_s", [P, N], U8)
+        steep_sb = held("steep_sb", [P, 2, PACK], F32)
+        share_sb = held("share_sb", [P, 2, PACK], F32)
+        lean_sb = held("lean_sb", [P, 2, PACK], F32)
+
+        nc.gpsimd.memset(tab_s[:].bitcast(I32), 0)
+        nc.gpsimd.memset(w2s_raw[:].rearrange("p a c -> p (a c)").bitcast(I32), 0)
+        nc.gpsimd.memset(v_s1[:].bitcast(I32), 0)
+        nc.gpsimd.memset(w4_s[:].bitcast(I32), 0)
+
+        def load_words(a):
+            nc.sync.dma_start(tab_w[a][:].bitcast(I32), tab_words[a].rearrange("p t i -> p (t i)").bitcast(I32))
+
+        def load_rows(name, rows):
+            raw = ring("raw", 4, name, [P, PACK, BANK], F32)
+            nc.sync.dma_start(raw[:], rows)
+            return raw
+
+        def four_rows(ap):
+            return ap.rearrange("(p j) c -> p j c", j=PACK)
+
+        nc.sync.dma_start(offs_sb[:], offs)
+        nc.sync.dma_start(pos2_sb[:], pos2)
+        load_words(0)
+        nc.sync.dma_start(w2_raw[:].bitcast(I32), w2_words.rearrange("a p c -> p a c").bitcast(I32))
+        for q in range(4):
+            nc.sync.dma_start(tab_s[32 * q : 32 * q + 8, :].bitcast(I32), tab_scales[:, 4 * q : 4 * q + 4, :].bitcast(I32))
+        load_words(1)
+        for q in range(4):
+            nc.sync.dma_start(
+                w2s_raw[32 * q : 32 * q + 4, :, :].bitcast(I32),
+                w2_scales[:, 4 * q : 4 * q + 4, :].rearrange("a r c -> r a c").bitcast(I32),
+            )
+        w1_raw = {}
+
+        def load_w1(b):
+            for a in range(2):
+                rows = w1[PASS * a : PASS * (a + 1), PASS * b : PASS * (b + 1)]
+                w1_raw[b, a] = load_rows("w1_raw%d%d" % (b, a), four_rows(rows))
+
+        load_w1(0)
+        nc.sync.dma_start(pos1_sb[:], pos1)
+        load_w1(1)
+        for vec_sb, vec in ((steep_sb, steep), (share_sb, share), (lean_sb, lean)):
+            nc.sync.dma_start(vec_sb[:], vec.rearrange("(b p i) -> p b i", b=2, i=PACK))
+        age_sb = []
+        for b in range(2):
+            age_b = held("age%d" % b, [P, PACK, M], F32)
+            nc.sync.dma_start(age_b[:], four_rows(age[PASS * b : PASS * (b + 1), :]))
+            age_sb.append(age_b)
+        w3_raw = [load_rows("w3_raw%d" % b, four_rows(w3[PASS * b : PASS * (b + 1), :])) for b in range(2)]
+        nc.sync.dma_start(w4_w[:].bitcast(I32), w4_words.rearrange("a p c i -> p a (c i)").bitcast(I32))
+        for q in range(4):
+            nc.sync.dma_start(w4_s[32 * q : 32 * q + 8, :].bitcast(I32), w4_scales[:, 4 * q : 4 * q + 4, :].bitcast(I32))
+        resid_sb = load_rows("resid_sb", resid.rearrange("(t p) m -> p t m", p=P))
+
+        nc.vector.tensor_copy(v_s[:], tab_s[:].indirect(offs_sb[:]))
+        nc.scalar.dma_start(v_s1[0:100, :].bitcast(I32), v_s[4:104, :].bitcast(I32))
+        v_w = [held("v_w0", [P, S], U32), ring("first", 1, "v_w1", [P, S], U32)]
+        nc.vector.tensor_copy(v_w[0][:], tab_w[0][:].indirect(offs_sb[:]))
+
+        w2_w, w2_s = [], []
+        for b in range(2):
+            words = held("w2_w%d" % b, [P, 2, 2 * PASS], U8)
+            nc.scalar.copy(
+                words[:].bitcast(U16).rearrange("p a (t m) -> p a t m", t=PACK),
+                w2_raw[:, :, 2 * PASS * b : 2 * PASS * (b + 1)].bitcast(U16).rearrange("p a (m t) -> p a t m", t=PACK),
+            )
+            w2_w.append(words)
+            w2_s.append(held("w2_s%d" % b, [P, 2, PASS], U8))
+
+        def deal_w2_scales(b):
+            nc.vector.tensor_copy(
+                w2_s[b][:].rearrange("p a (t m) -> p a t m", t=PACK),
+                w2s_raw[:, :, PASS * b : PASS * (b + 1)].rearrange("p a (m t) -> p a t m", t=PACK),
+            )
+
+        deal_w2_scales(0)
+        half = BANK // LANES
+        for u in range(2):
+            nc.vector.tensor_copy(
+                v_w[1][:, BANK * u : BANK * (u + 1)], tab_w[1][:].indirect(offs_sb[:, half * u : half * (u + 1)])
+            )
+        deal_w2_scales(1)
+
+        g_sb = {}
+
+        def atlas_tile(b, i):
+            tag = {(0, 0): "g00", (0, 1): "g01", (1, 0): "tops00", (1, 1): "tops01"}.get((b, i), "g%d%d" % (b, i))
+            g_sb[b, i] = ring(tag, 1, "g%d%d" % (b, i), [P, S], F32)
+            for u in range(2):
+                cols = slice(BANK * u, BANK * (u + 1))
+                acc = bank("to_scalar", "g_ps%d%d%d" % (b, i, u))
+                for a, plane in enumerate((v_s, v_s1)):
+                    nc.tensor.matmul_mx(
+                        out=acc[:],
+                        lhsT=w2_w[b][:, a, 2 * P * i : 2 * P * (i + 1)].bitcast(FP4X4),
+                        lhsT_scale=w2_s[b][:, a, P * i : P * (i + 1)],
+                        rhs=v_w[a][:, cols].bitcast(FP8X4),
+                        rhs_scale=plane[:, cols],
+                        start=(a == 0),
+                        stop=(a == 1),
+                    )
+                nc.scalar.copy(g_sb[b, i][:, cols], acc[:])
+
+        w1_w, w1_s = {}, {}
+
+        def quantise_w1(b):
+            grouped = [
+                ring("g00" if (b, a) == (1, 0) else "w1_g%d%d" % (b, a), 1, "w1_g%d%d" % (b, a), [P, PASS * PACK], BF16)
+                for a in range(2)
+            ]
+            (nc.vector.tensor_copy if b == 0 else nc.scalar.copy)(
+                grouped[0][:].rearrange("p (t m j) -> p m j t", t=PACK, j=PACK),
+                w1_raw[b, 0][:].rearrange("p j (m t) -> p m j t", t=PACK),
+            )
+            nc.gpsimd.tensor_scalar(
+                grouped[1][:].rearrange("p (t m j) -> p m t j", t=PACK, j=PACK),
+                w1_raw[b, 1][:].rearrange("p j (m t) -> p m t j", t=PACK),
+                1.0, 0.0, ALU.mult, ALU.add,
+            )
+            w1_w[b] = ring("g01" if b == 0 else "tops02", 1, "w1_w%d" % b, [P, 2 * PASS], U32)
+            w1_s[b] = held("w1_s%d" % b, [P, 2 * PASS], U8)
+            for a in range(2):
+                cols = slice(PASS * a, PASS * (a + 1))
+                nc.vector.quantize_mx(w1_w[b][:, cols].bitcast(FP8X4), w1_s[b][:, cols], grouped[a][:])
+
+        def weave(copy, dst, src):
+            copy(dst.rearrange("p (c j t) -> p c t j", j=4, t=PACK), src.rearrange("p t (c j) -> p c t j", j=4))
+
+        def quantise(name, copy, src, width):
+            grouped = held(name + "_g", [P, width * PACK], BF16)
+            weave(copy, grouped[:], src)
+            words = held(name + "_w", [P, width], U32)
+            plane = held(name + "_s", [P, width], U8)
+            nc.vector.quantize_mx(words[:].bitcast(FP8X4), plane[:], grouped[:])
+            return words, plane
+
+        slope = held("slope", [P, 2, PACK], F32)
+        bias = held("bias", [P, 2, PACK], F32)
+        x_sb = [held("x%d" % b, [P, PACK, M], F32) for b in range(2)]
+
+        def gated_age(b, i):
+            if (b, i) == (1, PACK - 1):
+                h_sb = ring("h_last", 1, "h_last", [P, S], F32)
+            else:
+                h_sb = ring("h", 5, "h%d%d" % (b, i), [P, S], F32)
+            tops = ring("tops%d%d" % (b, i), 1, "tops%d%d" % (b, i), [P, 2], F32)
+            for u in range(2):
+                cols = slice(BANK * u, BANK * (u + 1))
+                acc = bank("to_vector", "h_ps%d%d%d" % (b, i, u))
+                for a in range(2):
+                    w_cols = slice(PASS * a + P * i, PASS * a + P * (i + 1))
+                    nc.tensor.matmul_mx(
+                        out=acc[:],
+                        lhsT=w1_w[b][:, w_cols].bitcast(FP8X4),
+                        lhsT_scale=w1_s[b][:, w_cols],
+                        rhs=v_w[a][:, cols].bitcast(FP8X4),
+                        rhs_scale=v_s[4 * a :, cols],
+                        start=(a == 0),
+                        stop=(a == 1),
+                    )
+                nc.vector.tensor_scalar(
+                    h_sb[:, cols], acc[:], 1.0, None, ALU.mult, ALU.max, accum_out=tops[:, u : u + 1]
+                )
+            nc.vector.tensor_scalar(
+                bias[:, b, i : i + 1], tops[:, 0:1], tops[:, 1:2], slope[:, b, i : i + 1], ALU.max, ALU.mult
+            )
+            nc.scalar.activation(
+                out=x_sb[b][:, i, :], in_=h_sb[:].indirect(pos1_sb[:]), func=ACT.Sigmoid,
+                bias=bias[:, b, i : i + 1], scale=steep_sb[:, b, i : i + 1],
+            )
+            nc.gpsimd.tensor_tensor(x_sb[b][:, i, :], x_sb[b][:, i, :], age_sb[b][:, i, :], ALU.mult)
+
+        picked = {}
+
+        def pick(b, i, m0, m1):
+            nc.vector.tensor_copy(picked[b][:, i, m0:m1], g_sb[b, i][:].indirect(pos2_sb[:, m0 // LANES : m1 // LANES]))
+
+        def add_atlas(dst, b, i, m0, m1):
+            nc.vector.scalar_tensor_tensor(
+                dst[:, i, m0:m1], picked[b][:, i, m0:m1], lean_sb[:, b, i : i + 1], x_sb[b][:, i, m0:m1],
+                ALU.mult, ALU.add,
+            )
+
+        for i in range(PACK):
+            atlas_tile(0, i)
+        picked[0] = held("picked0", [P, PACK, M], F32)
+        for i in range(2):
+            pick(0, i, 0, M)
+        quantise_w1(0)
+        for i in range(2, PACK):
+            pick(0, i, 0, M)
+        nc.vector.scalar_tensor_tensor(slope[:], steep_sb[:], -1.0, share_sb[:], ALU.mult, ALU.mult)
+        for i in range(3):
+            gated_age(0, i)
+        quantise_w1(1)
+        gated_age(0, 3)
+        for i in range(PACK):
+            gated_age(1, i)
+        x0 = ring("tops10", 1, "x0_sum", [P, PACK, M], F32)
+        for i in range(PACK):
+            add_atlas(x0, 0, i, 0, M)
+        for i in range(PACK):
+            atlas_tile(1, i)
+        picked[1] = ring("tops13", 1, "picked1", [P, PACK, M], F32)
+        w3_g = ring("h_last", 1, "w3_g", [P, 2, N * PACK], BF16)
+        weave(nc.scalar.copy, w3_g[:, 0, :], w3_raw[0][:])
+        for u in range(4):
+            nc.gpsimd.tensor_scalar(
+                w3_g[:, 1, PASS * u : PASS * (u + 1)].rearrange("p (n j) -> p n j", j=PACK),
+                w3_raw[1][:, :, P * u : P * (u + 1)].rearrange("p j n -> p n j"),
+                1.0, 0.0, ALU.mult, ALU.add,
+            )
+        x0_w, x0_s = quantise("x0", nc.scalar.copy, x0[:], M)
+
+        def readings(m0, m1, x1_w, x1_s, c0, n_tiles):
+            width = m1 - m0
+            name = "%d_%d" % (m0, n_tiles[0])
+            y_ps, d_ps = bank("to_scalar", "y_ps" + name), bank("to_vector", "d_ps" + name)
+            x_parts = ((x0_w[:, m0:m1], x0_s[:, m0:m1]), (x1_w[:, m0 - c0 : m1 - c0], x1_s[:, m0 - c0 : m1 - c0]))
+            for b, (x_w, x_s) in enumerate(x_parts):
+                for acc, second in ((y_ps, False), (d_ps, True)):
+                    for e, nt in enumerate(n_tiles):
+                        n_cols = slice(P * nt, P * (nt + 1))
+                        nc.tensor.matmul_mx(
+                            out=acc[:, width * e : width * (e + 1)],
+                            lhsT=(w4_w[:, b, n_cols] if second else w3_w[:, b, n_cols]).bitcast(FP8X4),
+                            lhsT_scale=w4_s[4 * b :, n_cols] if second else w3_s[:, b, n_cols],
+                            rhs=x_w.bitcast(FP8X4),
+                            rhs_scale=x_s,
+                            start=(b == 0 and e == 0),
+                            stop=(b == 1 and e == len(n_tiles) - 1),
+                        )
+            res = held("res" + name, [P, BANK], F32)
+            nc.scalar.copy(res[:], y_ps[:])
+            nc.vector.tensor_tensor(res[:], d_ps[:], res[:], ALU.max)
+            rows = slice(n_tiles[0], n_tiles[-1] + 1)
+            res3 = res[:].rearrange("p (t m) -> p t m", m=width)
+            (nc.vector if m0 > 0 else nc.gpsimd).tensor_tensor(res3, res3, resid_sb[:, rows, m0:m1], ALU.subtract)
+            nc.sync.dma_start(out.rearrange("(t p) m -> p t m", p=P)[:, rows, m0:m1], res3)
+
+        for i in range(PACK):
+            pick(1, i, 0, WIDE)
+            add_atlas(x_sb[1], 1, i, 0, WIDE)
+        w3_w, w3_s = held("w3_w", [P, 2, N], U32), held("w3_s", [P, 2, N], U8)
+        for b in range(2):
+            nc.vector.quantize_mx(w3_w[:, b, :].bitcast(FP8X4), w3_s[:, b, :], w3_g[:, b, :])
+        xa_w, xa_s = quantise("x1a", nc.scalar.copy, x_sb[1][:, :, 0:WIDE], WIDE)
+        for i in range(PACK):
+            pick(1, i, WIDE, M)
+            add_atlas(x_sb[1], 1, i, WIDE, M)
+        xb_w, xb_s = quantise("x1b", nc.vector.tensor_copy, x_sb[1][:, :, WIDE:M], M - WIDE)
+        readings(0, 256, xa_w, xa_s, 0, (0, 1))
+        readings(0, 256, xa_w, xa_s, 0, (2, 3))
+        readings(256, WIDE, xa_w, xa_s, 0, (0, 1, 2, 3))
+        readings(WIDE, M, xb_w, xb_s, WIDE, (0, 1, 2, 3))

@@ -19,9 +19,18 @@ ACT = mybir.ActivationFunctionType
 P = 128
 PACK = 4
 PASS = P * PACK
+PASSES = 2
+QUADRANTS = 4
 BANK = 512
 LANES = 16
+LINE = 4
 WIDE = 384
+RAW_BUFS = 3
+H_BUFS = 5
+
+AFTER_PICK = "g%d%d"
+AFTER_MAX = "top%d%d"
+AFTER_LAST_LOOK = "h_last"
 
 
 def tile_list_bone_age_evidence_kernel(
@@ -29,16 +38,14 @@ def tile_list_bone_age_evidence_kernel(
     w3, w4_words, w4_scales, resid, out,
 ):
     nc = tc.nc
+    tiles = [(b, i) for b in range(PASSES) for i in range(PACK)]
     with ExitStack() as ctx:
         lists = ctx.enter_context(tc.tile_pool(name="lists", bufs=1))
         keep = ctx.enter_context(tc.tile_pool(name="keep", bufs=1))
         psum = ctx.enter_context(tc.psum_pool(name="psum", bufs=4))
 
-        def held(name, shape, dtype):
-            return keep.tile(shape, dtype, name=name, align_bytes=64)
-
-        def ring(tag, bufs, name, shape, dtype):
-            return keep.tile(shape, dtype, name=name, tag=tag, bufs=bufs, align_bytes=64)
+        def held(name, shape, dtype, tag=None, bufs=1):
+            return keep.tile(shape, dtype, name=name, tag=tag or name, bufs=bufs, align_bytes=64)
 
         def bank(tag, name):
             return psum.tile([P, BANK], F32, name=name, tag=tag)
@@ -47,267 +54,235 @@ def tile_list_bone_age_evidence_kernel(
         pos1_sb = lists.tile([P, M // LANES], U16, name="pos1_sb")
         pos2_sb = lists.tile([P, M // LANES], U16, name="pos2_sb")
 
-        tab_w = [held("tab_w%d" % a, [P, T], U32) for a in range(2)]
-        tab_s = ring("first", 1, "tab_s", [P, T], U8)
-        v_s = held("v_s", [P, S], U8)
-        v_s1 = held("v_s1", [P, S], U8)
-        w2_raw = held("w2_raw", [P, 2, 2 * H], U8)
-        w2s_raw = held("w2s_raw", [P, 2, H], U8)
-        w4_w = held("w4_w", [P, 2, N], U32)
+        tab_w = [held("tab_w%d" % a, [P, T], U32) for a in range(PASSES)]
+        tab_s = held("tab_s", [P, PASSES, T], U8)
+        w2_raw = held("w2_raw", [P, PASSES, 2 * H], U8)
+        w2s_raw = held("w2s_raw", [P, PASSES, H], U8)
+        w4_w = held("w4_w", [P, PASSES, N], U32)
         w4_s = held("w4_s", [P, N], U8)
-        steep_sb = held("steep_sb", [P, 2, PACK], F32)
-        share_sb = held("share_sb", [P, 2, PACK], F32)
-        lean_sb = held("lean_sb", [P, 2, PACK], F32)
+        steep_sb = held("steep_sb", [P, PASSES, PACK], F32)
+        share_sb = held("share_sb", [P, PASSES, PACK], F32)
+        lean_sb = held("lean_sb", [P, PASSES, PACK], F32)
 
-        nc.gpsimd.memset(tab_s[:].bitcast(I32), 0)
+        nc.gpsimd.memset(tab_s[:, 0, :].bitcast(I32), 0)
+        nc.vector.memset(tab_s[:, 1, :].bitcast(I32), 0)
         nc.gpsimd.memset(w2s_raw[:].rearrange("p a c -> p (a c)").bitcast(I32), 0)
-        nc.gpsimd.memset(v_s1[:].bitcast(I32), 0)
         nc.gpsimd.memset(w4_s[:].bitcast(I32), 0)
 
-        def load_words(a):
+        def load_table_words(a):
             nc.sync.dma_start(tab_w[a][:].bitcast(I32), tab_words[a].rearrange("p t i -> p (t i)").bitcast(I32))
 
-        def load_rows(name, rows):
-            raw = ring("raw", 4, name, [P, PACK, BANK], F32)
+        def load_planes_side_by_side(tile, scales):
+            for q in range(QUADRANTS):
+                nc.sync.dma_start(
+                    tile[32 * q : 32 * q + 4, :, :].bitcast(I32),
+                    scales[:, 4 * q : 4 * q + 4, :].rearrange("a s c -> s a c").bitcast(I32),
+                )
+
+        def load_raw(name, rows, tag="raw", bufs=RAW_BUFS):
+            raw = held(name, [P, PACK, BANK], F32, tag, bufs)
             nc.sync.dma_start(raw[:], rows)
             return raw
 
         def four_rows(ap):
             return ap.rearrange("(p j) c -> p j c", j=PACK)
 
+        def block(b):
+            return slice(PASS * b, PASS * (b + 1))
+
         nc.sync.dma_start(offs_sb[:], offs)
         nc.sync.dma_start(pos2_sb[:], pos2)
-        load_words(0)
+        load_table_words(0)
         nc.sync.dma_start(w2_raw[:].bitcast(I32), w2_words.rearrange("a p c -> p a c").bitcast(I32))
-        for q in range(4):
-            nc.sync.dma_start(tab_s[32 * q : 32 * q + 8, :].bitcast(I32), tab_scales[:, 4 * q : 4 * q + 4, :].bitcast(I32))
-        load_words(1)
-        for q in range(4):
-            nc.sync.dma_start(
-                w2s_raw[32 * q : 32 * q + 4, :, :].bitcast(I32),
-                w2_scales[:, 4 * q : 4 * q + 4, :].rearrange("a r c -> r a c").bitcast(I32),
-            )
-        w1_raw = {}
-
-        def load_w1(b):
-            for a in range(2):
-                rows = w1[PASS * a : PASS * (a + 1), PASS * b : PASS * (b + 1)]
-                w1_raw[b, a] = load_rows("w1_raw%d%d" % (b, a), four_rows(rows))
-
-        load_w1(0)
+        load_planes_side_by_side(tab_s, tab_scales)
+        load_table_words(1)
+        load_planes_side_by_side(w2s_raw, w2_scales)
+        w1_raw = {
+            (0, 0): load_raw("w1_raw00", four_rows(w1[block(0), block(0)]), AFTER_PICK % (0, 0), 1),
+            (0, 1): load_raw("w1_raw01", four_rows(w1[block(1), block(0)])),
+        }
         nc.sync.dma_start(pos1_sb[:], pos1)
-        load_w1(1)
+        for a in range(PASSES):
+            w1_raw[1, a] = load_raw("w1_raw1%d" % a, four_rows(w1[block(a), block(1)]))
         for vec_sb, vec in ((steep_sb, steep), (share_sb, share), (lean_sb, lean)):
-            nc.sync.dma_start(vec_sb[:], vec.rearrange("(b p i) -> p b i", b=2, i=PACK))
-        age_sb = []
-        for b in range(2):
-            age_b = held("age%d" % b, [P, PACK, M], F32)
-            nc.sync.dma_start(age_b[:], four_rows(age[PASS * b : PASS * (b + 1), :]))
-            age_sb.append(age_b)
-        w3_raw = [load_rows("w3_raw%d" % b, four_rows(w3[PASS * b : PASS * (b + 1), :])) for b in range(2)]
+            nc.sync.dma_start(vec_sb[:], vec.rearrange("(b p i) -> p b i", b=PASSES, i=PACK))
+        age_sb = [held("age%d" % b, [P, PACK, M], F32) for b in range(PASSES)]
+        for b in range(PASSES):
+            nc.sync.dma_start(age_sb[b][:], four_rows(age[block(b), :]))
+        w3_raw = [load_raw("w3_raw%d" % b, four_rows(w3[block(b), :])) for b in range(PASSES)]
         nc.sync.dma_start(w4_w[:].bitcast(I32), w4_words.rearrange("a p c i -> p a (c i)").bitcast(I32))
-        for q in range(4):
+        for q in range(QUADRANTS):
             nc.sync.dma_start(w4_s[32 * q : 32 * q + 8, :].bitcast(I32), w4_scales[:, 4 * q : 4 * q + 4, :].bitcast(I32))
-        resid_sb = load_rows("resid_sb", resid.rearrange("(t p) m -> p t m", p=P))
+        resid_sb = load_raw("resid_sb", resid.rearrange("(t p) m -> p t m", p=P))
 
-        nc.vector.tensor_copy(v_s[:], tab_s[:].indirect(offs_sb[:]))
-        nc.scalar.dma_start(v_s1[0:100, :].bitcast(I32), v_s[4:104, :].bitcast(I32))
-        v_w = [held("v_w0", [P, S], U32), ring("first", 1, "v_w1", [P, S], U32)]
+        v_w = [held("v_w%d" % a, [P, S], U32) for a in range(PASSES)]
+        v_s = [held("v_s%d" % a, [P, S], U8) for a in range(PASSES)]
+        w2_w = [held("w2_w%d" % b, [P, PASSES, 2 * PASS], U8) for b in range(PASSES)]
+        w2_s = [held("w2_s%d" % b, [P, PASSES, PASS], U8) for b in range(PASSES)]
+
+        def deal(copy, dst, src):
+            copy(dst.rearrange("p a (i m) -> p a i m", i=PACK), src.rearrange("p a (m i) -> p a i m", i=PACK))
+
         nc.vector.tensor_copy(v_w[0][:], tab_w[0][:].indirect(offs_sb[:]))
+        for a in range(PASSES):
+            nc.vector.tensor_copy(v_s[a][:], tab_s[:, a, :].indirect(offs_sb[:]))
+        for b in range(PASSES):
+            deal(nc.scalar.copy, w2_w[b][:].bitcast(U16), w2_raw[:, :, 2 * PASS * b : 2 * PASS * (b + 1)].bitcast(U16))
+        for u in range(S // BANK):
+            entries = offs_sb[:, BANK // LANES * u : BANK // LANES * (u + 1)]
+            nc.vector.tensor_copy(v_w[1][:, BANK * u : BANK * (u + 1)], tab_w[1][:].indirect(entries))
+            deal(nc.vector.tensor_copy, w2_s[u][:], w2s_raw[:, :, block(u)])
 
-        w2_w, w2_s = [], []
-        for b in range(2):
-            words = held("w2_w%d" % b, [P, 2, 2 * PASS], U8)
-            nc.scalar.copy(
-                words[:].bitcast(U16).rearrange("p a (t m) -> p a t m", t=PACK),
-                w2_raw[:, :, 2 * PASS * b : 2 * PASS * (b + 1)].bitcast(U16).rearrange("p a (m t) -> p a t m", t=PACK),
+        def first_stage(acc, cols, words, planes):
+            for a in range(PASSES):
+                nc.tensor.matmul_mx(
+                    out=acc[:], lhsT=words[a], lhsT_scale=planes[a],
+                    rhs=v_w[a][:, cols].bitcast(FP8X4), rhs_scale=v_s[a][:, cols],
+                    start=(a == 0), stop=(a == PASSES - 1),
+                )
+
+        def quantise(words, plane, woven):
+            nc.vector.quantize_mx(words.bitcast(FP8X4), plane, woven)
+
+        def weave(copy, dst, src):
+            copy(dst.rearrange("p (c j t) -> p c t j", j=LINE, t=PACK), src.rearrange("p t (c j) -> p c t j", j=LINE))
+
+        def weave_and_deal_w1(copy, b, a, tag):
+            woven = held("w1_g%d%d" % (b, a), [P, PASS * PACK], BF16, tag)
+            copy(
+                woven[:].rearrange("p (i m j) -> p m j i", i=PACK, j=PACK),
+                w1_raw[b, a][:].rearrange("p j (m i) -> p m j i", i=PACK),
             )
-            w2_w.append(words)
-            w2_s.append(held("w2_s%d" % b, [P, 2, PASS], U8))
-
-        def deal_w2_scales(b):
-            nc.vector.tensor_copy(
-                w2_s[b][:].rearrange("p a (t m) -> p a t m", t=PACK),
-                w2s_raw[:, :, PASS * b : PASS * (b + 1)].rearrange("p a (m t) -> p a t m", t=PACK),
-            )
-
-        deal_w2_scales(0)
-        half = BANK // LANES
-        for u in range(2):
-            nc.vector.tensor_copy(
-                v_w[1][:, BANK * u : BANK * (u + 1)], tab_w[1][:].indirect(offs_sb[:, half * u : half * (u + 1)])
-            )
-        deal_w2_scales(1)
-
-        g_sb = {}
-
-        def atlas_tile(b, i):
-            tag = {(0, 0): "g00", (0, 1): "g01", (1, 0): "tops00", (1, 1): "tops01"}.get((b, i), "g%d%d" % (b, i))
-            g_sb[b, i] = ring(tag, 1, "g%d%d" % (b, i), [P, S], F32)
-            for u in range(2):
-                cols = slice(BANK * u, BANK * (u + 1))
-                acc = bank("to_scalar", "g_ps%d%d%d" % (b, i, u))
-                for a, plane in enumerate((v_s, v_s1)):
-                    nc.tensor.matmul_mx(
-                        out=acc[:],
-                        lhsT=w2_w[b][:, a, 2 * P * i : 2 * P * (i + 1)].bitcast(FP4X4),
-                        lhsT_scale=w2_s[b][:, a, P * i : P * (i + 1)],
-                        rhs=v_w[a][:, cols].bitcast(FP8X4),
-                        rhs_scale=plane[:, cols],
-                        start=(a == 0),
-                        stop=(a == 1),
-                    )
-                nc.scalar.copy(g_sb[b, i][:, cols], acc[:])
+            return woven
 
         w1_w, w1_s = {}, {}
 
-        def quantise_w1(b):
-            grouped = [
-                ring("g00" if (b, a) == (1, 0) else "w1_g%d%d" % (b, a), 1, "w1_g%d%d" % (b, a), [P, PASS * PACK], BF16)
-                for a in range(2)
-            ]
-            (nc.vector.tensor_copy if b == 0 else nc.scalar.copy)(
-                grouped[0][:].rearrange("p (t m j) -> p m j t", t=PACK, j=PACK),
-                w1_raw[b, 0][:].rearrange("p j (m t) -> p m j t", t=PACK),
-            )
-            nc.gpsimd.tensor_scalar(
-                grouped[1][:].rearrange("p (t m j) -> p m t j", t=PACK, j=PACK),
-                w1_raw[b, 1][:].rearrange("p j (m t) -> p m t j", t=PACK),
-                1.0, 0.0, ALU.mult, ALU.add,
-            )
-            w1_w[b] = ring("g01" if b == 0 else "tops02", 1, "w1_w%d" % b, [P, 2 * PASS], U32)
-            w1_s[b] = held("w1_s%d" % b, [P, 2 * PASS], U8)
-            for a in range(2):
-                cols = slice(PASS * a, PASS * (a + 1))
-                nc.vector.quantize_mx(w1_w[b][:, cols].bitcast(FP8X4), w1_s[b][:, cols], grouped[a][:])
+        def quantise_w1(b, woven, tag):
+            w1_w[b] = held("w1_w%d" % b, [P, PASSES, PASS], U32, tag)
+            w1_s[b] = held("w1_s%d" % b, [P, PASSES, PASS], U8)
+            for a in range(PASSES):
+                quantise(w1_w[b][:, a, :], w1_s[b][:, a, :], woven[a][:])
 
-        def weave(copy, dst, src):
-            copy(dst.rearrange("p (c j t) -> p c t j", j=4, t=PACK), src.rearrange("p t (c j) -> p c t j", j=4))
+        g_sb = {}
+        picked = [held("picked%d" % b, [P, PACK, M], F32) for b in range(PASSES)]
 
-        def quantise(name, copy, src, width):
-            grouped = held(name + "_g", [P, width * PACK], BF16)
-            weave(copy, grouped[:], src)
-            words = held(name + "_w", [P, width], U32)
-            plane = held(name + "_s", [P, width], U8)
-            nc.vector.quantize_mx(words[:].bitcast(FP8X4), plane[:], grouped[:])
-            return words, plane
+        def atlas_tile(b, i):
+            g_sb[b, i] = held("g%d%d" % (b, i), [P, S], F32, AFTER_PICK % (b, i))
+            for u in range(S // BANK):
+                cols = slice(BANK * u, BANK * (u + 1))
+                acc = bank("to_scalar", "g_ps%d%d%d" % (b, i, u))
+                first_stage(
+                    acc, cols,
+                    [w2_w[b][:, a, 2 * P * i : 2 * P * (i + 1)].bitcast(FP4X4) for a in range(PASSES)],
+                    [w2_s[b][:, a, P * i : P * (i + 1)] for a in range(PASSES)],
+                )
+                nc.scalar.copy(g_sb[b, i][:, cols], acc[:])
 
-        slope = held("slope", [P, 2, PACK], F32)
-        bias = held("bias", [P, 2, PACK], F32)
-        x_sb = [held("x%d" % b, [P, PACK, M], F32) for b in range(2)]
+        def pick(b, i):
+            nc.vector.tensor_copy(picked[b][:, i, :], g_sb[b, i][:].indirect(pos2_sb[:]))
 
-        def gated_age(b, i):
-            if (b, i) == (1, PACK - 1):
-                h_sb = ring("h_last", 1, "h_last", [P, S], F32)
-            else:
-                h_sb = ring("h", 5, "h%d%d" % (b, i), [P, S], F32)
-            tops = ring("tops%d%d" % (b, i), 1, "tops%d%d" % (b, i), [P, 2], F32)
-            for u in range(2):
+        w1_g0 = [weave_and_deal_w1(nc.scalar.copy, 0, 0, None), weave_and_deal_w1(nc.vector.tensor_copy, 0, 1, None)]
+        for b, i in tiles:
+            atlas_tile(b, i)
+        for b, i in tiles[:-2]:
+            pick(b, i)
+        quantise_w1(0, w1_g0, AFTER_PICK % tiles[-3])
+        for b, i in tiles[-2:]:
+            pick(b, i)
+        w1_g1 = [weave_and_deal_w1(nc.scalar.copy, 1, a, AFTER_PICK % (0, a)) for a in range(PASSES)]
+        w3_g = [held("w3_g0", [P, N * PACK], BF16, AFTER_PICK % tiles[-2])]
+        weave(nc.scalar.copy, w3_g[0][:], w3_raw[0][:])
+
+        slope = held("slope", [P, PASSES, PACK], F32)
+        nc.vector.scalar_tensor_tensor(slope[:], steep_sb[:], -1.0, share_sb[:], ALU.mult, ALU.mult)
+        gate_sb = [held("gate%d" % b, [P, PACK, M], F32) for b in range(PASSES)]
+
+        def times_age(engine, b, i):
+            engine.tensor_tensor(gate_sb[b][:, i, :], gate_sb[b][:, i, :], age_sb[b][:, i, :], ALU.mult)
+
+        def look(b, i):
+            h_buffer = (AFTER_LAST_LOOK, 1) if (b, i) == tiles[-1] else ("h", H_BUFS)
+            h_sb = held("h%d%d" % (b, i), [P, S], F32, *h_buffer)
+            tops = held("top%d%d" % (b, i), [P, S // BANK], F32, AFTER_MAX % (b, i))
+            bias = held("bias%d%d" % (b, i), [P, 2], F32)
+            for u in range(S // BANK):
                 cols = slice(BANK * u, BANK * (u + 1))
                 acc = bank("to_vector", "h_ps%d%d%d" % (b, i, u))
-                for a in range(2):
-                    w_cols = slice(PASS * a + P * i, PASS * a + P * (i + 1))
-                    nc.tensor.matmul_mx(
-                        out=acc[:],
-                        lhsT=w1_w[b][:, w_cols].bitcast(FP8X4),
-                        lhsT_scale=w1_s[b][:, w_cols],
-                        rhs=v_w[a][:, cols].bitcast(FP8X4),
-                        rhs_scale=v_s[4 * a :, cols],
-                        start=(a == 0),
-                        stop=(a == 1),
-                    )
-                nc.vector.tensor_scalar(
-                    h_sb[:, cols], acc[:], 1.0, None, ALU.mult, ALU.max, accum_out=tops[:, u : u + 1]
+                first_stage(
+                    acc, cols,
+                    [w1_w[b][:, a, P * i : P * (i + 1)].bitcast(FP8X4) for a in range(PASSES)],
+                    [w1_s[b][:, a, P * i : P * (i + 1)] for a in range(PASSES)],
                 )
+                nc.vector.tensor_scalar(h_sb[:, cols], acc[:], 1.0, None, ALU.mult, ALU.max, accum_out=tops[:, u : u + 1])
             nc.vector.tensor_scalar(
-                bias[:, b, i : i + 1], tops[:, 0:1], tops[:, 1:2], slope[:, b, i : i + 1], ALU.max, ALU.mult
+                bias[:, 0:1], tops[:, 0:1], tops[:, 1:2], slope[:, b, i : i + 1], ALU.max, ALU.mult
             )
             nc.scalar.activation(
-                out=x_sb[b][:, i, :], in_=h_sb[:].indirect(pos1_sb[:]), func=ACT.Sigmoid,
-                bias=bias[:, b, i : i + 1], scale=steep_sb[:, b, i : i + 1],
+                out=gate_sb[b][:, i, :], in_=h_sb[:].indirect(pos1_sb[:]), func=ACT.Sigmoid,
+                bias=bias[:, 0:1], scale=steep_sb[:, b, i : i + 1],
             )
-            nc.gpsimd.tensor_tensor(x_sb[b][:, i, :], x_sb[b][:, i, :], age_sb[b][:, i, :], ALU.mult)
 
-        picked = {}
+        for b, i in tiles:
+            look(b, i)
+            if b == 0:
+                times_age(nc.gpsimd, b, i)
+            if (b, i) == tiles[1]:
+                quantise_w1(1, w1_g1, AFTER_MAX % (b, i))
+        w3_g.append(held("w3_g1", [P, N * PACK], BF16, AFTER_LAST_LOOK))
+        weave(nc.scalar.copy, w3_g[1][:], w3_raw[1][:])
 
-        def pick(b, i, m0, m1):
-            nc.vector.tensor_copy(picked[b][:, i, m0:m1], g_sb[b, i][:].indirect(pos2_sb[:, m0 // LANES : m1 // LANES]))
-
-        def add_atlas(dst, b, i, m0, m1):
+        def add_atlas(dst, b, i):
             nc.vector.scalar_tensor_tensor(
-                dst[:, i, m0:m1], picked[b][:, i, m0:m1], lean_sb[:, b, i : i + 1], x_sb[b][:, i, m0:m1],
-                ALU.mult, ALU.add,
+                dst[:, i, :], picked[b][:, i, :], lean_sb[:, b, i : i + 1], gate_sb[b][:, i, :], ALU.mult, ALU.add
             )
 
-        for i in range(PACK):
-            atlas_tile(0, i)
-        picked[0] = held("picked0", [P, PACK, M], F32)
-        for i in range(2):
-            pick(0, i, 0, M)
-        quantise_w1(0)
-        for i in range(2, PACK):
-            pick(0, i, 0, M)
-        nc.vector.scalar_tensor_tensor(slope[:], steep_sb[:], -1.0, share_sb[:], ALU.mult, ALU.mult)
-        for i in range(3):
-            gated_age(0, i)
-        quantise_w1(1)
-        gated_age(0, 3)
-        for i in range(PACK):
-            gated_age(1, i)
-        x0 = ring("tops10", 1, "x0_sum", [P, PACK, M], F32)
-        for i in range(PACK):
-            add_atlas(x0, 0, i, 0, M)
-        for i in range(PACK):
-            atlas_tile(1, i)
-        picked[1] = ring("tops13", 1, "picked1", [P, PACK, M], F32)
-        w3_g = ring("h_last", 1, "w3_g", [P, 2, N * PACK], BF16)
-        weave(nc.scalar.copy, w3_g[:, 0, :], w3_raw[0][:])
-        for u in range(4):
-            nc.gpsimd.tensor_scalar(
-                w3_g[:, 1, PASS * u : PASS * (u + 1)].rearrange("p (n j) -> p n j", j=PACK),
-                w3_raw[1][:, :, P * u : P * (u + 1)].rearrange("p j n -> p n j"),
-                1.0, 0.0, ALU.mult, ALU.add,
+        def mx_tiles(name, width):
+            return (
+                held(name + "_g", [P, width * PACK], BF16), held(name + "_w", [P, width], U32), held(name + "_s", [P, width], U8)
             )
-        x0_w, x0_s = quantise("x0", nc.scalar.copy, x0[:], M)
 
-        def readings(m0, m1, x1_w, x1_s, c0, n_tiles):
+        x_sb = [held("x0", [P, PACK, M], F32, AFTER_MAX % tiles[-1]), gate_sb[1]]
+        for i in range(PACK):
+            add_atlas(x_sb[0], 0, i)
+        for i in range(PACK):
+            times_age(nc.vector, 1, i)
+        w3_w, w3_s = held("w3_w", [P, PASSES, N], U32), held("w3_s", [P, PASSES, N], U8)
+        quantise(w3_w[:, 0, :], w3_s[:, 0, :], w3_g[0][:])
+        for i in range(PACK):
+            add_atlas(x_sb[1], 1, i)
+        x0_g, x0_w, x0_s = mx_tiles("x0", M)
+        wide_g, wide_w, wide_s = mx_tiles("x1_wide", WIDE)
+        rest_g, rest_w, rest_s = mx_tiles("x1_rest", M - WIDE)
+        weave(nc.scalar.copy, x0_g[:], x_sb[0][:])
+        weave(nc.scalar.copy, wide_g[:], x_sb[1][:, :, 0:WIDE])
+        quantise(x0_w[:], x0_s[:], x0_g[:])
+        weave(nc.vector.tensor_copy, rest_g[:], x_sb[1][:, :, WIDE:M])
+        quantise(w3_w[:, 1, :], w3_s[:, 1, :], w3_g[1][:])
+        quantise(rest_w[:], rest_s[:], rest_g[:])
+        quantise(wide_w[:], wide_s[:], wide_g[:])
+
+        def readings(m0, m1, x1_w, x1_s, row_tiles, subtract_on):
             width = m1 - m0
-            name = "%d_%d" % (m0, n_tiles[0])
+            name = "%d_%d" % (m0, row_tiles[0])
             y_ps, d_ps = bank("to_scalar", "y_ps" + name), bank("to_vector", "d_ps" + name)
-            x_parts = ((x0_w[:, m0:m1], x0_s[:, m0:m1]), (x1_w[:, m0 - c0 : m1 - c0], x1_s[:, m0 - c0 : m1 - c0]))
-            for b, (x_w, x_s) in enumerate(x_parts):
-                for acc, second in ((y_ps, False), (d_ps, True)):
-                    for e, nt in enumerate(n_tiles):
-                        n_cols = slice(P * nt, P * (nt + 1))
+            for b, (x_w, x_s) in enumerate(((x0_w[:, m0:m1], x0_s[:, m0:m1]), (x1_w, x1_s))):
+                for acc, w_w, w_s in ((d_ps, w4_w[:, b, :], w4_s[4 * b :, :]), (y_ps, w3_w[:, b, :], w3_s[:, b, :])):
+                    for e, t in enumerate(row_tiles):
                         nc.tensor.matmul_mx(
                             out=acc[:, width * e : width * (e + 1)],
-                            lhsT=(w4_w[:, b, n_cols] if second else w3_w[:, b, n_cols]).bitcast(FP8X4),
-                            lhsT_scale=w4_s[4 * b :, n_cols] if second else w3_s[:, b, n_cols],
-                            rhs=x_w.bitcast(FP8X4),
-                            rhs_scale=x_s,
-                            start=(b == 0 and e == 0),
-                            stop=(b == 1 and e == len(n_tiles) - 1),
+                            lhsT=w_w[:, P * t : P * (t + 1)].bitcast(FP8X4), lhsT_scale=w_s[:, P * t : P * (t + 1)],
+                            rhs=x_w.bitcast(FP8X4), rhs_scale=x_s,
+                            start=(b == 0 and e == 0), stop=(b == PASSES - 1 and e == len(row_tiles) - 1),
                         )
             res = held("res" + name, [P, BANK], F32)
             nc.scalar.copy(res[:], y_ps[:])
             nc.vector.tensor_tensor(res[:], d_ps[:], res[:], ALU.max)
-            rows = slice(n_tiles[0], n_tiles[-1] + 1)
-            res3 = res[:].rearrange("p (t m) -> p t m", m=width)
-            (nc.vector if m0 > 0 else nc.gpsimd).tensor_tensor(res3, res3, resid_sb[:, rows, m0:m1], ALU.subtract)
-            nc.sync.dma_start(out.rearrange("(t p) m -> p t m", p=P)[:, rows, m0:m1], res3)
+            rows = slice(row_tiles[0], row_tiles[-1] + 1)
+            res_t = res[:].rearrange("p (t m) -> p t m", m=width)
+            subtract_on.tensor_tensor(res_t, res_t, resid_sb[:, rows, m0:m1], ALU.subtract)
+            nc.sync.dma_start(out.rearrange("(t p) m -> p t m", p=P)[:, rows, m0:m1], res_t)
 
-        for i in range(PACK):
-            pick(1, i, 0, WIDE)
-            add_atlas(x_sb[1], 1, i, 0, WIDE)
-        w3_w, w3_s = held("w3_w", [P, 2, N], U32), held("w3_s", [P, 2, N], U8)
-        for b in range(2):
-            nc.vector.quantize_mx(w3_w[:, b, :].bitcast(FP8X4), w3_s[:, b, :], w3_g[:, b, :])
-        xa_w, xa_s = quantise("x1a", nc.scalar.copy, x_sb[1][:, :, 0:WIDE], WIDE)
-        for i in range(PACK):
-            pick(1, i, WIDE, M)
-            add_atlas(x_sb[1], 1, i, WIDE, M)
-        xb_w, xb_s = quantise("x1b", nc.vector.tensor_copy, x_sb[1][:, :, WIDE:M], M - WIDE)
-        readings(0, 256, xa_w, xa_s, 0, (0, 1))
-        readings(0, 256, xa_w, xa_s, 0, (2, 3))
-        readings(256, WIDE, xa_w, xa_s, 0, (0, 1, 2, 3))
-        readings(WIDE, M, xb_w, xb_s, WIDE, (0, 1, 2, 3))
+        readings(WIDE, M, rest_w[:], rest_s[:], (0, 1, 2, 3), nc.gpsimd)
+        readings(0, 256, wide_w[:, 0:256], wide_s[:, 0:256], (0, 1), nc.gpsimd)
+        readings(0, 256, wide_w[:, 0:256], wide_s[:, 0:256], (2, 3), nc.vector)
+        readings(256, WIDE, wide_w[:, 256:WIDE], wide_s[:, 256:WIDE], (0, 1, 2, 3), nc.vector)

from contextlib import ExitStack

import concourse.mybir as mybir

K, T, S, M, H, N = 1024, 2048, 1024, 512, 1024, 512
FLOPS = 2 * (2 * K * H * S + 2 * H * N * M)

F32 = mybir.dt.float32
BF16 = mybir.dt.bfloat16
I32 = mybir.dt.int32
U32 = mybir.dt.uint32
U16 = mybir.dt.uint16
U8 = mybir.dt.uint8
FP8X4 = mybir.dt.float8_e4m3fn_x4
FP4X4 = mybir.dt.float4_e2m1fn_x4
ALU = mybir.AluOpType
ACT = mybir.ActivationFunctionType

P = 128
PACK = 4
PASS = P * PACK
PASSES = 2
QUADRANTS = 4
BANK = 512
LANES = 16
LINE = 4
WIDE = 384
RAW_BUFS = 3
H_BUFS = 5

AFTER_PICK = "g%d%d"
AFTER_MAX = "top%d%d"
AFTER_LAST_LOOK = "h_last"


def tile_list_bone_age_evidence_kernel(
    tc, tab_words, tab_scales, offs, pos1, pos2, w1, w2_words, w2_scales, steep, share, age, lean,
    w3, w4_words, w4_scales, resid, out,
):
    nc = tc.nc
    tiles = [(b, i) for b in range(PASSES) for i in range(PACK)]
    with ExitStack() as ctx:
        lists = ctx.enter_context(tc.tile_pool(name="lists", bufs=1))
        keep = ctx.enter_context(tc.tile_pool(name="keep", bufs=1))
        psum = ctx.enter_context(tc.psum_pool(name="psum", bufs=4))

        def held(name, shape, dtype, tag=None, bufs=1):
            return keep.tile(shape, dtype, name=name, tag=tag or name, bufs=bufs, align_bytes=64)

        def bank(tag, name):
            return psum.tile([P, BANK], F32, name=name, tag=tag)

        offs_sb = lists.tile([P, S // LANES], U16, name="offs_sb")
        pos1_sb = lists.tile([P, M // LANES], U16, name="pos1_sb")
        pos2_sb = lists.tile([P, M // LANES], U16, name="pos2_sb")

        tab_w = [held("tab_w%d" % a, [P, T], U32) for a in range(PASSES)]
        tab_s = held("tab_s", [P, PASSES, T], U8)
        w2_raw = held("w2_raw", [P, PASSES, 2 * H], U8)
        w2s_raw = held("w2s_raw", [P, PASSES, H], U8)
        w4_w = held("w4_w", [P, PASSES, N], U32)
        w4_s = held("w4_s", [P, N], U8)
        steep_sb = held("steep_sb", [P, PASSES, PACK], F32)
        share_sb = held("share_sb", [P, PASSES, PACK], F32)
        lean_sb = held("lean_sb", [P, PASSES, PACK], F32)

        nc.gpsimd.memset(tab_s[:, 0, :].bitcast(I32), 0)
        nc.vector.memset(tab_s[:, 1, :].bitcast(I32), 0)
        nc.gpsimd.memset(w2s_raw[:].rearrange("p a c -> p (a c)").bitcast(I32), 0)
        nc.gpsimd.memset(w4_s[:].bitcast(I32), 0)

        def load_table_words(a):
            nc.sync.dma_start(tab_w[a][:].bitcast(I32), tab_words[a].rearrange("p t i -> p (t i)").bitcast(I32))

        def load_planes_side_by_side(tile, scales):
            for q in range(QUADRANTS):
                nc.sync.dma_start(
                    tile[32 * q : 32 * q + 4, :, :].bitcast(I32),
                    scales[:, 4 * q : 4 * q + 4, :].rearrange("a s c -> s a c").bitcast(I32),
                )

        def load_raw(name, rows, tag="raw", bufs=RAW_BUFS):
            raw = held(name, [P, PACK, BANK], F32, tag, bufs)
            nc.sync.dma_start(raw[:], rows)
            return raw

        def four_rows(ap):
            return ap.rearrange("(p j) c -> p j c", j=PACK)

        def block(b):
            return slice(PASS * b, PASS * (b + 1))

        nc.sync.dma_start(offs_sb[:], offs)
        nc.sync.dma_start(pos2_sb[:], pos2)
        load_table_words(0)
        nc.sync.dma_start(w2_raw[:].bitcast(I32), w2_words.rearrange("a p c -> p a c").bitcast(I32))
        load_planes_side_by_side(tab_s, tab_scales)
        load_table_words(1)
        load_planes_side_by_side(w2s_raw, w2_scales)
        w1_raw = {
            (0, 0): load_raw("w1_raw00", four_rows(w1[block(0), block(0)]), AFTER_PICK % (0, 0), 1),
            (0, 1): load_raw("w1_raw01", four_rows(w1[block(1), block(0)])),
        }
        nc.sync.dma_start(pos1_sb[:], pos1)
        for a in range(PASSES):
            w1_raw[1, a] = load_raw("w1_raw1%d" % a, four_rows(w1[block(a), block(1)]))
        for vec_sb, vec in ((steep_sb, steep), (share_sb, share), (lean_sb, lean)):
            nc.sync.dma_start(vec_sb[:], vec.rearrange("(b p i) -> p b i", b=PASSES, i=PACK))
        age_sb = [held("age%d" % b, [P, PACK, M], F32) for b in range(PASSES)]
        for b in range(PASSES):
            nc.sync.dma_start(age_sb[b][:], four_rows(age[block(b), :]))
        w3_raw = [load_raw("w3_raw%d" % b, four_rows(w3[block(b), :])) for b in range(PASSES)]
        nc.sync.dma_start(w4_w[:].bitcast(I32), w4_words.rearrange("a p c i -> p a (c i)").bitcast(I32))
        for q in range(QUADRANTS):
            nc.sync.dma_start(w4_s[32 * q : 32 * q + 8, :].bitcast(I32), w4_scales[:, 4 * q : 4 * q + 4, :].bitcast(I32))
        resid_sb = load_raw("resid_sb", resid.rearrange("(t p) m -> p t m", p=P))

        v_w = [held("v_w%d" % a, [P, S], U32) for a in range(PASSES)]
        v_s = [held("v_s%d" % a, [P, S], U8) for a in range(PASSES)]
        w2_w = [held("w2_w%d" % b, [P, PASSES, 2 * PASS], U8) for b in range(PASSES)]
        w2_s = [held("w2_s%d" % b, [P, PASSES, PASS], U8) for b in range(PASSES)]

        def deal(copy, dst, src):
            copy(dst.rearrange("p a (i m) -> p a i m", i=PACK), src.rearrange("p a (m i) -> p a i m", i=PACK))

        nc.vector.tensor_copy(v_w[0][:], tab_w[0][:].indirect(offs_sb[:]))
        for a in range(PASSES):
            nc.vector.tensor_copy(v_s[a][:], tab_s[:, a, :].indirect(offs_sb[:]))
        for b in range(PASSES):
            deal(nc.scalar.copy, w2_w[b][:].bitcast(U16), w2_raw[:, :, 2 * PASS * b : 2 * PASS * (b + 1)].bitcast(U16))
        for u in range(S // BANK):
            entries = offs_sb[:, BANK // LANES * u : BANK // LANES * (u + 1)]
            nc.vector.tensor_copy(v_w[1][:, BANK * u : BANK * (u + 1)], tab_w[1][:].indirect(entries))
            deal(nc.vector.tensor_copy, w2_s[u][:], w2s_raw[:, :, block(u)])

        def first_stage(acc, cols, words, planes):
            for a in range(PASSES):
                nc.tensor.matmul_mx(
                    out=acc[:], lhsT=words[a], lhsT_scale=planes[a],
                    rhs=v_w[a][:, cols].bitcast(FP8X4), rhs_scale=v_s[a][:, cols],
                    start=(a == 0), stop=(a == PASSES - 1),
                )

        def quantise(words, plane, woven):
            nc.vector.quantize_mx(words.bitcast(FP8X4), plane, woven)

        def weave(copy, dst, src):
            copy(dst.rearrange("p (c j t) -> p c t j", j=LINE, t=PACK), src.rearrange("p t (c j) -> p c t j", j=LINE))

        def weave_and_deal_w1(copy, b, a, tag):
            woven = held("w1_g%d%d" % (b, a), [P, PASS * PACK], BF16, tag)
            copy(
                woven[:].rearrange("p (i m j) -> p m j i", i=PACK, j=PACK),
                w1_raw[b, a][:].rearrange("p j (m i) -> p m j i", i=PACK),
            )
            return woven

        w1_w, w1_s = {}, {}

        def quantise_w1(b, woven, tag):
            w1_w[b] = held("w1_w%d" % b, [P, PASSES, PASS], U32, tag)
            w1_s[b] = held("w1_s%d" % b, [P, PASSES, PASS], U8)
            for a in range(PASSES):
                quantise(w1_w[b][:, a, :], w1_s[b][:, a, :], woven[a][:])

        g_sb = {}
        picked = [held("picked%d" % b, [P, PACK, M], F32) for b in range(PASSES)]

        def atlas_tile(b, i):
            g_sb[b, i] = held("g%d%d" % (b, i), [P, S], F32, AFTER_PICK % (b, i))
            for u in range(S // BANK):
                cols = slice(BANK * u, BANK * (u + 1))
                acc = bank("to_scalar", "g_ps%d%d%d" % (b, i, u))
                first_stage(
                    acc, cols,
                    [w2_w[b][:, a, 2 * P * i : 2 * P * (i + 1)].bitcast(FP4X4) for a in range(PASSES)],
                    [w2_s[b][:, a, P * i : P * (i + 1)] for a in range(PASSES)],
                )
                nc.scalar.copy(g_sb[b, i][:, cols], acc[:])

        def pick(b, i):
            nc.vector.tensor_copy(picked[b][:, i, :], g_sb[b, i][:].indirect(pos2_sb[:]))

        w1_g0 = [weave_and_deal_w1(nc.scalar.copy, 0, 0, None), weave_and_deal_w1(nc.vector.tensor_copy, 0, 1, None)]
        for b, i in tiles:
            atlas_tile(b, i)
        for b, i in tiles[:-2]:
            pick(b, i)
        quantise_w1(0, w1_g0, AFTER_PICK % tiles[-3])
        for b, i in tiles[-2:]:
            pick(b, i)
        w1_g1 = [weave_and_deal_w1(nc.scalar.copy, 1, a, AFTER_PICK % (0, a)) for a in range(PASSES)]
        w3_g = [held("w3_g0", [P, N * PACK], BF16, AFTER_PICK % tiles[-2])]
        weave(nc.scalar.copy, w3_g[0][:], w3_raw[0][:])

        slope = held("slope", [P, PASSES, PACK], F32)
        nc.vector.scalar_tensor_tensor(slope[:], steep_sb[:], -1.0, share_sb[:], ALU.mult, ALU.mult)
        gate_sb = [held("gate%d" % b, [P, PACK, M], F32) for b in range(PASSES)]

        def times_age(engine, b, i):
            engine.tensor_tensor(gate_sb[b][:, i, :], gate_sb[b][:, i, :], age_sb[b][:, i, :], ALU.mult)

        def look(b, i):
            h_buffer = (AFTER_LAST_LOOK, 1) if (b, i) == tiles[-1] else ("h", H_BUFS)
            h_sb = held("h%d%d" % (b, i), [P, S], F32, *h_buffer)
            tops = held("top%d%d" % (b, i), [P, S // BANK], F32, AFTER_MAX % (b, i))
            bias = held("bias%d%d" % (b, i), [P, 2], F32)
            for u in range(S // BANK):
                cols = slice(BANK * u, BANK * (u + 1))
                acc = bank("to_vector", "h_ps%d%d%d" % (b, i, u))
                first_stage(
                    acc, cols,
                    [w1_w[b][:, a, P * i : P * (i + 1)].bitcast(FP8X4) for a in range(PASSES)],
                    [w1_s[b][:, a, P * i : P * (i + 1)] for a in range(PASSES)],
                )
                nc.vector.tensor_scalar(h_sb[:, cols], acc[:], 1.0, None, ALU.mult, ALU.max, accum_out=tops[:, u : u + 1])
            nc.vector.tensor_scalar(
                bias[:, 0:1], tops[:, 0:1], tops[:, 1:2], slope[:, b, i : i + 1], ALU.max, ALU.mult
            )
            nc.scalar.activation(
                out=gate_sb[b][:, i, :], in_=h_sb[:].indirect(pos1_sb[:]), func=ACT.Sigmoid,
                bias=bias[:, 0:1], scale=steep_sb[:, b, i : i + 1],
            )

        for b, i in tiles:
            look(b, i)
            if b == 0:
                times_age(nc.gpsimd, b, i)
            if (b, i) == tiles[1]:
                quantise_w1(1, w1_g1, AFTER_MAX % (b, i))
        w3_g.append(held("w3_g1", [P, N * PACK], BF16, AFTER_LAST_LOOK))
        weave(nc.scalar.copy, w3_g[1][:], w3_raw[1][:])

        def add_atlas(dst, b, i):
            nc.vector.scalar_tensor_tensor(
                dst[:, i, :], picked[b][:, i, :], lean_sb[:, b, i : i + 1], gate_sb[b][:, i, :], ALU.mult, ALU.add
            )

        def mx_tiles(name, width):
            return (
                held(name + "_g", [P, width * PACK], BF16), held(name + "_w", [P, width], U32), held(name + "_s", [P, width], U8)
            )

        x_sb = [held("x0", [P, PACK, M], F32, AFTER_MAX % tiles[-1]), gate_sb[1]]
        for i in range(PACK):
            add_atlas(x_sb[0], 0, i)
        for i in range(PACK):
            times_age(nc.vector, 1, i)
        w3_w, w3_s = held("w3_w", [P, PASSES, N], U32), held("w3_s", [P, PASSES, N], U8)
        quantise(w3_w[:, 0, :], w3_s[:, 0, :], w3_g[0][:])
        for i in range(PACK):
            add_atlas(x_sb[1], 1, i)
        x0_g, x0_w, x0_s = mx_tiles("x0", M)
        wide_g, wide_w, wide_s = mx_tiles("x1_wide", WIDE)
        rest_g, rest_w, rest_s = mx_tiles("x1_rest", M - WIDE)
        weave(nc.scalar.copy, x0_g[:], x_sb[0][:])
        weave(nc.scalar.copy, wide_g[:], x_sb[1][:, :, 0:WIDE])
        quantise(x0_w[:], x0_s[:], x0_g[:])
        weave(nc.vector.tensor_copy, rest_g[:], x_sb[1][:, :, WIDE:M])
        quantise(w3_w[:, 1, :], w3_s[:, 1, :], w3_g[1][:])
        quantise(rest_w[:], rest_s[:], rest_g[:])
        quantise(wide_w[:], wide_s[:], wide_g[:])

        def readings(m0, m1, x1_w, x1_s, row_tiles, subtract_on):
            width = m1 - m0
            name = "%d_%d" % (m0, row_tiles[0])
            y_ps, d_ps = bank("to_scalar", "y_ps" + name), bank("to_vector", "d_ps" + name)
            for b, (x_w, x_s) in enumerate(((x0_w[:, m0:m1], x0_s[:, m0:m1]), (x1_w, x1_s))):
                for acc, w_w, w_s in ((d_ps, w4_w[:, b, :], w4_s[4 * b :, :]), (y_ps, w3_w[:, b, :], w3_s[:, b, :])):
                    for e, t in enumerate(row_tiles):
                        nc.tensor.matmul_mx(
                            out=acc[:, width * e : width * (e + 1)],
                            lhsT=w_w[:, P * t : P * (t + 1)].bitcast(FP8X4), lhsT_scale=w_s[:, P * t : P * (t + 1)],
                            rhs=x_w.bitcast(FP8X4), rhs_scale=x_s,
                            start=(b == 0 and e == 0), stop=(b == PASSES - 1 and e == len(row_tiles) - 1),
                        )
            res = held("res" + name, [P, BANK], F32)
            nc.scalar.copy(res[:], y_ps[:])
            nc.vector.tensor_tensor(res[:], d_ps[:], res[:], ALU.max)
            rows = slice(row_tiles[0], row_tiles[-1] + 1)
            res_t = res[:].rearrange("p (t m) -> p t m", m=width)
            subtract_on.tensor_tensor(res_t, res_t, resid_sb[:, rows, m0:m1], ALU.subtract)
            nc.sync.dma_start(out.rearrange("(t p) m -> p t m", p=P)[:, rows, m0:m1], res_t)

        readings(WIDE, M, rest_w[:], rest_s[:], (0, 1, 2, 3), nc.gpsimd)
        readings(0, 256, wide_w[:, 0:256], wide_s[:, 0:256], (0, 1), nc.gpsimd)
        readings(0, 256, wide_w[:, 0:256], wide_s[:, 0:256], (2, 3), nc.vector)
        readings(256, WIDE, wide_w[:, 256:WIDE], wide_s[:, 256:WIDE], (0, 1, 2, 3), nc.vector)
